import numpy as np
import ml_dtypes


def mxq(x, axis, fmt="e4m3"):
    dtype, down = {"e4m3": (ml_dtypes.float8_e4m3fn, 7), "e5m2": (ml_dtypes.float8_e5m2, 14)}[fmt]
    v = np.moveaxis(np.asarray(x, np.float32).astype(ml_dtypes.bfloat16).astype(np.float64), axis, -1)
    blocks = v.reshape(v.shape[:-1] + (-1, 32))
    amax = np.abs(blocks).max(-1, keepdims=True)
    byte = np.maximum(np.where(amax > 0, np.frexp(amax)[1] - 1 + 127, 0) - down, 1)
    scale = np.exp2(byte - 127.0)
    codes = (blocks / scale).astype(np.float32).astype(dtype).astype(np.float64)
    return np.moveaxis((codes * scale).reshape(v.shape), -1, axis)


WIDE = False


def mx_kscale(k):
    if not WIDE:
        return np.ones(k)
    levels = np.array([10, -10, 5, -5, 0])
    if k % 512:
        return np.exp2(np.random.permutation(np.resize(levels, k // 32))).repeat(32)
    a = np.empty((k // 512, 16))
    for p in range(k // 512):
        a[p, :8] = np.random.permutation(np.resize(levels, 8))
        for g in range(8):
            far = levels[np.abs(levels - a[p, g]) >= 10]
            a[p, g + 8] = far[np.random.randint(len(far))]
    return np.exp2(a.ravel()).repeat(32)


def f64(x):
    return np.asarray(x).astype(np.float64)


def striped(idx):
    return np.tile(idx.reshape(-1, 16).T, (8, 1)).astype(np.uint16)


def unstriped(offs):
    return offs[:16].T.reshape(-1).astype(np.int64)


def striped8(idx):
    return np.concatenate([x.reshape(-1, 16).T for x in idx]).astype(np.uint16)


def runs(offs, k):
    lists = np.stack([offs[16 * r : 16 * r + 16].T.reshape(-1) for r in range(8)]).astype(np.int64)
    return lists[np.arange(k) % 512 // 64]


def pack_weight(w):
    k, n = w.shape
    w = f64(np.asarray(w, np.float32).astype(ml_dtypes.bfloat16)).reshape(k // 32, 32, n)
    amax = np.abs(w).max(1)
    byte = np.clip(np.where(amax > 0, np.frexp(amax)[1] - 1 + 127 - 7, 1), 1, 254)
    scaled = (w * np.exp2(127.0 - byte)[:, None, :]).reshape(k, n).astype(np.float32)
    words = np.ascontiguousarray(scaled.reshape(k // 512, 128, 4, n).transpose(0, 1, 3, 2)).astype(ml_dtypes.float8_e4m3fn).view(np.uint8)
    return words, np.ascontiguousarray(byte.astype(np.uint8).reshape(k // 512, 16, n))


def unpack_weight(words, scales):
    g, p, n, _ = words.shape
    vals = np.ascontiguousarray(words).view(ml_dtypes.float8_e4m3fn).astype(np.float64) * np.repeat(np.exp2(scales.astype(np.float64) - 127.0), 8, axis=1)[..., None]
    return vals.transpose(0, 1, 3, 2).reshape(g * 512, n)


K, T, S, H, C = 512, 2048, 512, 512, 512


def setup_inputs():
    n = np.random.standard_normal
    s = mx_kscale(K)[:, None]
    packed_xT = pack_weight(n((K, T)) * s)
    return {
        "x_words": packed_xT[0],
        "x_scales": packed_xT[1],
        "w1": (n((K, H)) / np.sqrt(K) / s).astype(np.float32),
        "gs": (np.random.uniform(0.5, 1.5, (K, 1)) / s).astype(np.float32),
        "offs": striped(np.random.permutation(T)[:S]),
        "n1": striped8(np.stack([np.random.permutation(S) for _ in range(8)])),
        "n2": striped8(np.stack([np.random.permutation(S) for _ in range(8)])),
        "cand": striped(np.random.permutation(T)[:C]),
    }


def reference(x_words, x_scales, w1, gs, offs, n1, n2, cand):
    x_cand = unpack_weight(x_words, x_scales)[:, unstriped(cand)]
    xq = unpack_weight(x_words, x_scales)[:, unstriped(offs)]
    h = mxq(f64(w1), 0, "e4m3").T @ xq
    th = np.tanh(h)
    z = f64(gs) * (th * (th[np.arange(H)[:, None], runs(n1, H)]) + 0.5 * (th[np.arange(H)[:, None], runs(n2, H)]))
    return 0.0625 * ((x_cand.T @ mxq(z, 0, "e4m3")))

@@ -1,0 +1,205 @@
+from contextlib import ExitStack
+
+import concourse.mybir as mybir
+
+K, T, S, H, C = 512, 2048, 512, 512, 512
+FLOPS = 2 * K * H * S + 2 * K * C * S
+
+F32 = mybir.dt.float32
+BF16 = mybir.dt.bfloat16
+I32 = mybir.dt.int32
+U32 = mybir.dt.uint32
+U16 = mybir.dt.uint16
+U8 = mybir.dt.uint8
+FP8X4 = mybir.dt.float8_e4m3fn_x4
+ACT = mybir.ActivationFunctionType
+ALU = mybir.AluOpType
+
+P = 128
+PACK = 4
+LIST_ROWS = 16
+CHUNKS = ((0, 256), (256, 128), (384, 128))
+MODES = ("V","V","Q","R")
+RING = 2
+
+
+def tile_picked_candtanh_none_p_kernel(tc, x_words, x_scales, w1, gs, offs, n1, n2, cand, out):
+    nc = tc.nc
+    with ExitStack() as ctx:
+        keep = ctx.enter_context(tc.tile_pool(name="keep", bufs=1))
+        psum = ctx.enter_context(tc.psum_pool(name="psum", bufs=1))
+
+        offs_sb = keep.tile([P, S // LIST_ROWS], U16, name="offs_sb")
+        cand_sb = keep.tile([P, C // LIST_ROWS], U16, name="cand_sb")
+        n1_sb = keep.tile([P, S // LIST_ROWS], U16, name="n1_sb")
+        n2_sb = keep.tile([P, S // LIST_ROWS], U16, name="n2_sb")
+        x_word_table = keep.tile([P, T], U32, name="x_word_table", align_bytes=64)
+        x_scale_table = keep.tile([P, T], U8, name="x_scale_table", align_bytes=64)
+        gs_sb = keep.tile([P, PACK], F32, name="gs_sb")
+        gs_half = keep.tile([P, PACK], F32, name="gs_half")
+        warm = keep.tile([P, 1], F32, name="warm")
+        warm_out = keep.tile([P, 1], F32, name="warm_out")
+        w_raw = [keep.tile([P, PACK, H // 2], F32, name="w_raw%d" % half) for half in range(2)]
+
+        nc.vector.memset(x_scale_table[:].bitcast(I32), 0)
+        nc.vector.memset(warm[:], 0.0)
+        nc.sync.dma_start(offs_sb[:], offs)
+        nc.sync.dma_start(cand_sb[:], cand)
+        nc.sync.dma_start(gs_sb[:], gs.rearrange("(p t) o -> p (t o)", t=PACK))
+        nc.sync.dma_start(n1_sb[:], n1)
+        nc.sync.dma_start(n2_sb[:], n2)
+        for quad in range(4):
+            nc.scalar.dma_start(
+                x_scale_table[32 * quad : 32 * quad + 4, :].bitcast(I32),
+                x_scales[0, 4 * quad : 4 * quad + 4, :].bitcast(I32),
+            )
+        w_rows = w1.rearrange("(p j) c -> p j c", j=PACK)
+        for half in range(2):
+            nc.sync.dma_start(w_raw[half][:], w_rows[:, :, half * (H // 2) : (half + 1) * (H // 2)])
+        nc.sync.dma_start(x_word_table[:].bitcast(I32), x_words[0].rearrange("p n t -> p (n t)").bitcast(I32))
+        nc.scalar.activation(warm_out[:], warm[:], ACT.Sigmoid)
+        nc.gpsimd.tensor_scalar(gs_half[:], gs_sb[:], 0.5, 0.0, ALU.mult, ALU.add)
+
+        pick_words = keep.tile([P, S], U32, name="pick_words", align_bytes=64)
+        pick_scales = keep.tile([P, S], U8, name="pick_scales", align_bytes=64)
+        cand_words = keep.tile([P, C], U32, name="cand_words", align_bytes=64)
+        cand_scales = keep.tile([P, C], U8, name="cand_scales", align_bytes=64)
+        nc.vector.tensor_copy(pick_scales[:], x_scale_table[:].indirect(offs_sb[:]))
+        nc.vector.tensor_copy(cand_scales[:], x_scale_table[:].indirect(cand_sb[:]))
+
+        w_grouped = keep.tile([P, PACK, P, PACK], BF16, name="w_grouped", align_bytes=64)
+        for half in range(2):
+            src = w_raw[half][:].rearrange("p j (m t) -> p m j t", t=PACK)
+            dst = w_grouped[:, :, half * (P // 2) : (half + 1) * (P // 2), :].rearrange("p t m j -> p m j t")
+            if half == 0:
+                nc.scalar.copy(dst, src)
+            else:
+                nc.vector.tensor_copy(dst, src)
+        w_codes = keep.tile([P, H], U32, name="w_codes", align_bytes=64)
+        w_scales = keep.tile([P, H], U8, name="w_scales", align_bytes=64)
+        nc.vector.quantize_mx(
+            out=w_codes[:].bitcast(FP8X4), scales=w_scales[:], in_=w_grouped[:].rearrange("p t m j -> p (t m j)")
+        )
+
+        for half in range(2):
+            cols = slice(half * (S // 2), (half + 1) * (S // 2))
+            lcols = slice(half * (S // 2) // LIST_ROWS, (half + 1) * (S // 2) // LIST_ROWS)
+            nc.vector.tensor_copy(pick_words[:, cols], x_word_table[:].indirect(offs_sb[:, lcols]))
+        nc.vector.tensor_copy(cand_words[:], x_word_table[:].indirect(cand_sb[:]))
+
+        th, gth, h2 = [], {}, {}
+        for t in range(PACK):
+            h_ps = psum.tile([P, S], F32, name="h_ps%d" % t, tag="bank%d" % t)
+            nc.tensor.matmul_mx(
+                out=h_ps[:],
+                lhsT=w_codes[:, t * P : (t + 1) * P].bitcast(FP8X4),
+                lhsT_scale=w_scales[:, t * P : (t + 1) * P],
+                rhs=pick_words[:].bitcast(FP8X4),
+                rhs_scale=pick_scales[:],
+                start=True,
+                stop=True,
+            )
+            th.append(keep.tile([P, S], F32, name="th%d" % t))
+            if MODES[t] != "V":
+                h2[t] = keep.tile([P, S], F32, name="h2_%d" % t)
+                nc.scalar.activation(h2[t][:], h_ps[:], ACT.Copy, scale=2.0)
+            nc.scalar.activation(th[t][:], h_ps[:], ACT.Tanh)
+
+        z_planes = [keep.tile([P, PACK, width], F32, name="z_planes%d" % c) for c, (j0, width) in enumerate(CHUNKS)]
+        got1 = [keep.tile([P, 256], F32, name="got1_%d" % i) for i in range(RING)]
+        got2 = [keep.tile([P, 256], F32, name="got2_%d" % i) for i in range(RING)]
+        prod = [keep.tile([P, 256], F32, name="prod%d" % i) for i in range(RING)]
+        out_rows = out.rearrange("(b p) j -> p b j", p=P)
+
+        def fetch(step, t, c):
+            j0, width = CHUNKS[c]
+            lcols = slice(j0 // LIST_ROWS, (j0 + width) // LIST_ROWS)
+            if MODES[t] == "V":
+                a, b = got1[step % RING], got2[step % RING]
+            else:
+                a = keep.tile([P, width], F32, name="sig1_%d_%d" % (t, c))
+                b = keep.tile([P, width], F32, name="sig2_%d_%d" % (t, c)) if MODES[t] == "R" else got2[step % RING]
+            if MODES[t] == "V":
+                nc.vector.tensor_copy(a[:, :width], th[t][:].indirect(n1_sb[:, lcols]))
+            else:
+                nc.scalar.activation(a[:, :width], h2[t][:].indirect(n1_sb[:, lcols]), ACT.Sigmoid)
+            if MODES[t] != "R":
+                nc.vector.tensor_copy(b[:, :width], th[t][:].indirect(n2_sb[:, lcols]))
+            else:
+                nc.scalar.activation(b[:, :width], h2[t][:].indirect(n2_sb[:, lcols]), ACT.Sigmoid)
+            if MODES[t] != "V" and c == 0:
+                gth[t] = keep.tile([P, S], F32, name="gth%d" % t)
+                nc.vector.tensor_scalar(gth[t][:], th[t][:], gs_sb[:, t : t + 1], 2.0, ALU.mult, ALU.mult)
+            return a, b
+
+        def first_term(step, t, c, a, b):
+            j0, width = CHUNKS[c]
+            u = prod[step % RING]
+            if MODES[t] == "V":
+                nc.vector.scalar_tensor_tensor(
+                    u[:, :width], a[:, :width], gs_sb[:, t : t + 1], th[t][:, j0 : j0 + width], ALU.mult, ALU.mult
+                )
+            else:
+                nc.vector.scalar_tensor_tensor(
+                    u[:, :width], a[:, :width], 0.5, gth[t][:, j0 : j0 + width], ALU.subtract, ALU.mult
+                )
+            if MODES[t] == "R":
+                b2 = got2[step % RING]
+                nc.vector.tensor_scalar(b2[:, :width], b[:, :width], 0.5, gs_sb[:, t : t + 1], ALU.subtract, ALU.mult)
+
+        def second_term(step, t, c, a, b):
+            j0, width = CHUNKS[c]
+            u = prod[step % RING]
+            if MODES[t] == "R":
+                nc.vector.tensor_tensor(z_planes[c][:, t, :], got2[step % RING][:, :width], u[:, :width], ALU.add)
+            else:
+                nc.vector.scalar_tensor_tensor(
+                    z_planes[c][:, t, :], b[:, :width], gs_half[:, t : t + 1], u[:, :width], ALU.mult, ALU.add
+                )
+
+        def score(c):
+            j0, width = CHUNKS[c]
+            last = c == len(CHUNKS) - 1
+            z_grouped = keep.tile([P, width, PACK], BF16, name="z_grouped%d" % c, align_bytes=64)
+            dst = z_grouped[:].rearrange("p (g i) t -> p g t i", i=4)
+            src = z_planes[c][:].rearrange("p t (g i) -> p g t i", i=4)
+            if last:
+                nc.vector.tensor_copy(dst, src)
+            else:
+                nc.scalar.copy(dst, src)
+            z_codes = keep.tile([P, width], U32, name="z_codes%d" % c, align_bytes=64)
+            z_scales = keep.tile([P, width], U8, name="z_scales%d" % c, align_bytes=64)
+            nc.vector.quantize_mx(
+                out=z_codes[:].bitcast(FP8X4), scales=z_scales[:], in_=z_grouped[:].rearrange("p n t -> p (n t)")
+            )
+            for pair in range(2):
+                acc = psum.tile([P, 2, width], F32, name="acc%d_%d" % (c, pair), tag="bank%d" % ((4 + 2 * c + pair) % 8))
+                for i in range(2):
+                    b = 2 * pair + i
+                    nc.tensor.matmul_mx(
+                        out=acc[:, i, :],
+                        lhsT=cand_words[:, b * P : (b + 1) * P].bitcast(FP8X4),
+                        lhsT_scale=cand_scales[:, b * P : (b + 1) * P],
+                        rhs=z_codes[:].bitcast(FP8X4),
+                        rhs_scale=z_scales[:],
+                        start=True,
+                        stop=True,
+                    )
+                res = keep.tile([P, 2, width], F32, name="res%d_%d" % (c, pair))
+                if last and pair == 1:
+                    nc.vector.tensor_scalar(res[:], acc[:], 0.0625, None, ALU.mult)
+                else:
+                    nc.scalar.activation(res[:], acc[:], ACT.Copy, scale=0.0625)
+                nc.sync.dma_start(out_rows[:, 2 * pair : 2 * pair + 2, j0 : j0 + width], res[:])
+
+        steps = [(t, c) for c in range(len(CHUNKS)) for t in range(PACK)]
+        got = fetch(0, *steps[0])
+        for step, (t, c) in enumerate(steps):
+            first_term(step, t, c, *got)
+            mine = got
+            if step + 1 < len(steps):
+                got = fetch(step + 1, *steps[step + 1])
+            second_term(step, t, c, *mine)
+            if t == 0 and c > 0:
+                score(c - 1)
+        score(len(CHUNKS) - 1)

@@ -19,8 +19,6 @@ P = 128
 PACK = 4
 LIST_ROWS = 16
 CHUNKS = ((0, 256), (256, 128), (384, 128))
-MODES = ("V","V","Q","R")
-RING = 2
 
 
 def tile_picked_candtanh_none_p_kernel(tc, x_words, x_scales, w1, gs, offs, n1, n2, cand, out):
@@ -45,19 +43,19 @@ def tile_picked_candtanh_none_p_kernel(tc, x_words, x_scales, w1, gs, offs, n1, 
         nc.vector.memset(warm[:], 0.0)
         nc.sync.dma_start(offs_sb[:], offs)
         nc.sync.dma_start(cand_sb[:], cand)
-        nc.sync.dma_start(gs_sb[:], gs.rearrange("(p t) o -> p (t o)", t=PACK))
-        nc.sync.dma_start(n1_sb[:], n1)
-        nc.sync.dma_start(n2_sb[:], n2)
+        w_rows = w1.rearrange("(p j) c -> p j c", j=PACK)
+        nc.sync.dma_start(w_raw[0][:], w_rows[:, :, : H // 2])
         for quad in range(4):
-            nc.scalar.dma_start(
+            nc.sync.dma_start(
                 x_scale_table[32 * quad : 32 * quad + 4, :].bitcast(I32),
                 x_scales[0, 4 * quad : 4 * quad + 4, :].bitcast(I32),
             )
-        w_rows = w1.rearrange("(p j) c -> p j c", j=PACK)
-        for half in range(2):
-            nc.sync.dma_start(w_raw[half][:], w_rows[:, :, half * (H // 2) : (half + 1) * (H // 2)])
+        nc.sync.dma_start(w_raw[1][:], w_rows[:, :, H // 2 :])
         nc.sync.dma_start(x_word_table[:].bitcast(I32), x_words[0].rearrange("p n t -> p (n t)").bitcast(I32))
-        nc.scalar.activation(warm_out[:], warm[:], ACT.Sigmoid)
+        nc.sync.dma_start(gs_sb[:], gs.rearrange("(p t) o -> p (t o)", t=PACK))
+        nc.sync.dma_start(n1_sb[:], n1)
+        nc.sync.dma_start(n2_sb[:], n2)
+        nc.scalar.activation(warm_out[:], warm[:], ACT.Tanh)
         nc.gpsimd.tensor_scalar(gs_half[:], gs_sb[:], 0.5, 0.0, ALU.mult, ALU.add)
 
         pick_words = keep.tile([P, S], U32, name="pick_words", align_bytes=64)
@@ -71,10 +69,7 @@ def tile_picked_candtanh_none_p_kernel(tc, x_words, x_scales, w1, gs, offs, n1, 
         for half in range(2):
             src = w_raw[half][:].rearrange("p j (m t) -> p m j t", t=PACK)
             dst = w_grouped[:, :, half * (P // 2) : (half + 1) * (P // 2), :].rearrange("p t m j -> p m j t")
-            if half == 0:
-                nc.scalar.copy(dst, src)
-            else:
-                nc.vector.tensor_copy(dst, src)
+            nc.scalar.copy(dst, src)
         w_codes = keep.tile([P, H], U32, name="w_codes", align_bytes=64)
         w_scales = keep.tile([P, H], U8, name="w_scales", align_bytes=64)
         nc.vector.quantize_mx(
@@ -87,82 +82,66 @@ def tile_picked_candtanh_none_p_kernel(tc, x_words, x_scales, w1, gs, offs, n1, 
             nc.vector.tensor_copy(pick_words[:, cols], x_word_table[:].indirect(offs_sb[:, lcols]))
         nc.vector.tensor_copy(cand_words[:], x_word_table[:].indirect(cand_sb[:]))
 
-        th, gth, h2 = [], {}, {}
-        for t in range(PACK):
-            h_ps = psum.tile([P, S], F32, name="h_ps%d" % t, tag="bank%d" % t)
+        th = [keep.tile([P, S], F32, name="th%d" % t) for t in range(PACK)]
+        gth = [keep.tile([P, S], F32, name="gth%d" % t) for t in range(PACK)]
+        hth = [keep.tile([P, S], F32, name="hth%d" % t) for t in range(PACK)]
+
+        def project(t, j0, width, bank):
+            h_ps = psum.tile([P, width], F32, name="h_ps%d_%d" % (t, j0), tag="bank%d" % bank)
             nc.tensor.matmul_mx(
                 out=h_ps[:],
                 lhsT=w_codes[:, t * P : (t + 1) * P].bitcast(FP8X4),
                 lhsT_scale=w_scales[:, t * P : (t + 1) * P],
-                rhs=pick_words[:].bitcast(FP8X4),
-                rhs_scale=pick_scales[:],
+                rhs=pick_words[:, j0 : j0 + width].bitcast(FP8X4),
+                rhs_scale=pick_scales[:, j0 : j0 + width],
                 start=True,
                 stop=True,
             )
-            th.append(keep.tile([P, S], F32, name="th%d" % t))
-            if MODES[t] != "V":
-                h2[t] = keep.tile([P, S], F32, name="h2_%d" % t)
-                nc.scalar.activation(h2[t][:], h_ps[:], ACT.Copy, scale=2.0)
-            nc.scalar.activation(th[t][:], h_ps[:], ACT.Tanh)
+            nc.scalar.activation(th[t][:, j0 : j0 + width], h_ps[:], ACT.Tanh)
 
-        z_planes = [keep.tile([P, PACK, width], F32, name="z_planes%d" % c) for c, (j0, width) in enumerate(CHUNKS)]
-        got1 = [keep.tile([P, 256], F32, name="got1_%d" % i) for i in range(RING)]
-        got2 = [keep.tile([P, 256], F32, name="got2_%d" % i) for i in range(RING)]
-        prod = [keep.tile([P, 256], F32, name="prod%d" % i) for i in range(RING)]
+        def weigh(dst, t, j0, width, factor):
+            nc.scalar.activation(dst[t][:, j0 : j0 + width], th[t][:, j0 : j0 + width], ACT.Copy, scale=factor[:, t : t + 1])
+
+        for half in range(2):
+            project(0, half * (S // 2), S // 2, 4 * half)
+            weigh(gth, 0, half * (S // 2), S // 2, gs_sb)
+        for t in range(1, PACK):
+            project(t, 0, S, t)
+            weigh(hth, t - 1, 0, S, gs_half)
+            weigh(gth, t, 0, S, gs_sb)
+        weigh(hth, PACK - 1, 0, S, gs_half)
+
+        z_half = [keep.tile([P, PACK, S // 2], F32, name="z_half%d" % half) for half in range(2)]
+        ring = [keep.tile([P, S // 2], F32, name="prod%d" % i) for i in range(2)]
+        prod = {}
         out_rows = out.rearrange("(b p) j -> p b j", p=P)
 
-        def fetch(step, t, c):
-            j0, width = CHUNKS[c]
+        def z_view(j0, width):
+            half, first = divmod(j0, S // 2)
+            return z_half[half][:, :, first : first + width]
+
+        def first_term(step, t, j0, width):
             lcols = slice(j0 // LIST_ROWS, (j0 + width) // LIST_ROWS)
-            if MODES[t] == "V":
-                a, b = got1[step % RING], got2[step % RING]
+            if j0 == CHUNKS[-1][0]:
+                prod[step] = keep.tile([P, width], F32, name="late%d" % t, tag="z_grouped%d" % (t - 2), align_bytes=64)
             else:
-                a = keep.tile([P, width], F32, name="sig1_%d_%d" % (t, c))
-                b = keep.tile([P, width], F32, name="sig2_%d_%d" % (t, c)) if MODES[t] == "R" else got2[step % RING]
-            if MODES[t] == "V":
-                nc.vector.tensor_copy(a[:, :width], th[t][:].indirect(n1_sb[:, lcols]))
-            else:
-                nc.scalar.activation(a[:, :width], h2[t][:].indirect(n1_sb[:, lcols]), ACT.Sigmoid)
-            if MODES[t] != "R":
-                nc.vector.tensor_copy(b[:, :width], th[t][:].indirect(n2_sb[:, lcols]))
-            else:
-                nc.scalar.activation(b[:, :width], h2[t][:].indirect(n2_sb[:, lcols]), ACT.Sigmoid)
-            if MODES[t] != "V" and c == 0:
-                gth[t] = keep.tile([P, S], F32, name="gth%d" % t)
-                nc.vector.tensor_scalar(gth[t][:], th[t][:], gs_sb[:, t : t + 1], 2.0, ALU.mult, ALU.mult)
-            return a, b
+                prod[step] = ring[step % 2]
+            nc.vector.tensor_tensor(
+                prod[step][:, :width], th[t][:].indirect(n1_sb[:, lcols]), gth[t][:, j0 : j0 + width], ALU.mult
+            )
 
-        def first_term(step, t, c, a, b):
-            j0, width = CHUNKS[c]
-            u = prod[step % RING]
-            if MODES[t] == "V":
-                nc.vector.scalar_tensor_tensor(
-                    u[:, :width], a[:, :width], gs_sb[:, t : t + 1], th[t][:, j0 : j0 + width], ALU.mult, ALU.mult
-                )
-            else:
-                nc.vector.scalar_tensor_tensor(
-                    u[:, :width], a[:, :width], 0.5, gth[t][:, j0 : j0 + width], ALU.subtract, ALU.mult
-                )
-            if MODES[t] == "R":
-                b2 = got2[step % RING]
-                nc.vector.tensor_scalar(b2[:, :width], b[:, :width], 0.5, gs_sb[:, t : t + 1], ALU.subtract, ALU.mult)
-
-        def second_term(step, t, c, a, b):
-            j0, width = CHUNKS[c]
-            u = prod[step % RING]
-            if MODES[t] == "R":
-                nc.vector.tensor_tensor(z_planes[c][:, t, :], got2[step % RING][:, :width], u[:, :width], ALU.add)
-            else:
-                nc.vector.scalar_tensor_tensor(
-                    z_planes[c][:, t, :], b[:, :width], gs_half[:, t : t + 1], u[:, :width], ALU.mult, ALU.add
-                )
+        def second_term(step, t, j0, width):
+            lcols = slice(j0 // LIST_ROWS, (j0 + width) // LIST_ROWS)
+            nc.vector.tensor_tensor(
+                z_view(j0, width)[:, t, :], hth[t][:].indirect(n2_sb[:, lcols]), prod[step][:, :width], ALU.add
+            )
 
         def score(c):
             j0, width = CHUNKS[c]
             last = c == len(CHUNKS) - 1
-            z_grouped = keep.tile([P, width, PACK], BF16, name="z_grouped%d" % c, align_bytes=64)
+            z_grouped = keep.tile([P, width, PACK], BF16, name="z_grouped%d" % c, tag="z_grouped%d" % c, align_bytes=64)
             dst = z_grouped[:].rearrange("p (g i) t -> p g t i", i=4)
-            src = z_planes[c][:].rearrange("p t (g i) -> p g t i", i=4)
+            src = z_view(j0, width).rearrange("p t (g i) -> p g t i", i=4)
             if last:
                 nc.vector.tensor_copy(dst, src)
             else:
@@ -173,7 +152,7 @@ def tile_picked_candtanh_none_p_kernel(tc, x_words, x_scales, w1, gs, offs, n1, 
                 out=z_codes[:].bitcast(FP8X4), scales=z_scales[:], in_=z_grouped[:].rearrange("p n t -> p (n t)")
             )
             for pair in range(2):
-                acc = psum.tile([P, 2, width], F32, name="acc%d_%d" % (c, pair), tag="bank%d" % ((4 + 2 * c + pair) % 8))
+                acc = psum.tile([P, 2, width], F32, name="acc%d_%d" % (c, pair), tag="bank%d" % ((5 + 2 * c + pair) % 8))
                 for i in range(2):
                     b = 2 * pair + i
                     nc.tensor.matmul_mx(
@@ -192,14 +171,15 @@ def tile_picked_candtanh_none_p_kernel(tc, x_words, x_scales, w1, gs, offs, n1, 
                     nc.scalar.activation(res[:], acc[:], ACT.Copy, scale=0.0625)
                 nc.sync.dma_start(out_rows[:, 2 * pair : 2 * pair + 2, j0 : j0 + width], res[:])
 
-        steps = [(t, c) for c in range(len(CHUNKS)) for t in range(PACK)]
-        got = fetch(0, *steps[0])
-        for step, (t, c) in enumerate(steps):
-            first_term(step, t, c, *got)
-            mine = got
-            if step + 1 < len(steps):
-                got = fetch(step + 1, *steps[step + 1])
-            second_term(step, t, c, *mine)
-            if t == 0 and c > 0:
-                score(c - 1)
-        score(len(CHUNKS) - 1)
+        steps = [(t, half * (S // 2), S // 2) for t in (0, 1) for half in range(2)]
+        steps = steps + [(t, j0, width) for j0, width in CHUNKS for t in (2, 3)]
+        first_term(0, *steps[0])
+        for step, (t, j0, width) in enumerate(steps):
+            if t == PACK - 1:
+                second_term(step, t, j0, width)
+                score(CHUNKS.index((j0, width)))
+                if step + 1 < len(steps):
+                    first_term(step + 1, *steps[step + 1])
+            else:
+                first_term(step + 1, *steps[step + 1])
+                second_term(step, t, j0, width)

@@ -55,8 +55,9 @@ def tile_picked_candtanh_none_p_kernel(tc, x_words, x_scales, w1, gs, offs, n1, 
         nc.sync.dma_start(gs_sb[:], gs.rearrange("(p t) o -> p (t o)", t=PACK))
         nc.sync.dma_start(n1_sb[:], n1)
         nc.sync.dma_start(n2_sb[:], n2)
-        nc.scalar.activation(warm_out[:], warm[:], ACT.Tanh)
-        nc.gpsimd.tensor_scalar(gs_half[:], gs_sb[:], 0.5, 0.0, ALU.mult, ALU.add)
+        nc.scalar.activation(warm_out[:], warm[:], ACT.Sigmoid)
+        nc.scalar.activation(gs_half[:, :2], gs_sb[:, :2], ACT.Copy, scale=0.5)
+        nc.scalar.activation(gs_half[:, 2:], gs_sb[:, 2:], ACT.Copy, scale=2.0)
 
         pick_words = keep.tile([P, S], U32, name="pick_words", align_bytes=64)
         pick_scales = keep.tile([P, S], U8, name="pick_scales", align_bytes=64)
@@ -82,9 +83,9 @@ def tile_picked_candtanh_none_p_kernel(tc, x_words, x_scales, w1, gs, offs, n1, 
             nc.vector.tensor_copy(pick_words[:, cols], x_word_table[:].indirect(offs_sb[:, lcols]))
         nc.vector.tensor_copy(cand_words[:], x_word_table[:].indirect(cand_sb[:]))
 
-        th = [keep.tile([P, S], F32, name="th%d" % t) for t in range(PACK)]
-        gth = [keep.tile([P, S], F32, name="gth%d" % t) for t in range(PACK)]
-        hth = [keep.tile([P, S], F32, name="hth%d" % t) for t in range(PACK)]
+        th = [keep.tile([P, S], F32, name="th%d" % t) for t in range(2)]
+        th_pair = keep.tile([P, 2, S], F32, name="th_pair")
+        h2 = [keep.tile([P, S], F32, name="h2_%d" % i) for i in range(2)]
 
         def project(t, j0, width, bank):
             h_ps = psum.tile([P, width], F32, name="h_ps%d_%d" % (t, j0), tag="bank%d" % bank)
@@ -97,51 +98,68 @@ def tile_picked_candtanh_none_p_kernel(tc, x_words, x_scales, w1, gs, offs, n1, 
                 start=True,
                 stop=True,
             )
-            nc.scalar.activation(th[t][:, j0 : j0 + width], h_ps[:], ACT.Tanh)
-
-        def weigh(dst, t, j0, width, factor):
-            nc.scalar.activation(dst[t][:, j0 : j0 + width], th[t][:, j0 : j0 + width], ACT.Copy, scale=factor[:, t : t + 1])
+            if t < 2:
+                nc.scalar.activation(th[t][:, j0 : j0 + width], h_ps[:], ACT.Tanh)
+            else:
+                nc.scalar.activation(h2[t - 2][:], h_ps[:], ACT.Copy, scale=2.0)
+                nc.scalar.activation(th_pair[:, t - 2, :], h_ps[:], ACT.Tanh)
 
         for half in range(2):
             project(0, half * (S // 2), S // 2, 4 * half)
-            weigh(gth, 0, half * (S // 2), S // 2, gs_sb)
         for t in range(1, PACK):
             project(t, 0, S, t)
-            weigh(hth, t - 1, 0, S, gs_half)
-            weigh(gth, t, 0, S, gs_sb)
-        weigh(hth, PACK - 1, 0, S, gs_half)
 
-        z_half = [keep.tile([P, PACK, S // 2], F32, name="z_half%d" % half) for half in range(2)]
-        ring = [keep.tile([P, S // 2], F32, name="prod%d" % i) for i in range(2)]
-        prod = {}
+        z_planes = [keep.tile([P, PACK, width], F32, name="z_planes%d" % c, tag="z_planes%d" % c) for c, (j0, width) in enumerate(CHUNKS)]
         out_rows = out.rearrange("(b p) j -> p b j", p=P)
 
-        def z_view(j0, width):
-            half, first = divmod(j0, S // 2)
-            return z_half[half][:, :, first : first + width]
+        def list_cols(c):
+            j0, width = CHUNKS[c]
+            return slice(j0 // LIST_ROWS, (j0 + width) // LIST_ROWS)
 
-        def first_term(step, t, j0, width):
-            lcols = slice(j0 // LIST_ROWS, (j0 + width) // LIST_ROWS)
-            if j0 == CHUNKS[-1][0]:
-                prod[step] = keep.tile([P, width], F32, name="late%d" % t, tag="z_grouped%d" % (t - 2), align_bytes=64)
-            else:
-                prod[step] = ring[step % 2]
-            nc.vector.tensor_tensor(
-                prod[step][:, :width], th[t][:].indirect(n1_sb[:, lcols]), gth[t][:, j0 : j0 + width], ALU.mult
-            )
+        def fetch_th(t, c, tags):
+            width = CHUNKS[c][1]
+            got = []
+            for lst, tag in zip((n1_sb, n2_sb), tags):
+                got.append(keep.tile([P, width], F32, name="got_" + tag, tag=tag))
+                nc.vector.tensor_copy(got[-1][:], th[t][:].indirect(lst[:, list_cols(c)]))
+            return got
 
-        def second_term(step, t, j0, width):
-            lcols = slice(j0 // LIST_ROWS, (j0 + width) // LIST_ROWS)
-            nc.vector.tensor_tensor(
-                z_view(j0, width)[:, t, :], hth[t][:].indirect(n2_sb[:, lcols]), prod[step][:, :width], ALU.add
-            )
+        def first_term(t, c, got):
+            j0, width = CHUNKS[c]
+            prod = keep.tile([P, width], F32, name="prod%d_%d" % (t, c))
+            nc.vector.scalar_tensor_tensor(prod[:], got[0][:], gs_sb[:, t : t + 1], th[t][:, j0 : j0 + width], ALU.mult, ALU.mult)
+            return prod
+
+        def second_term(t, c, got, prod):
+            nc.vector.scalar_tensor_tensor(z_planes[c][:, t, :], got[1][:], gs_half[:, t : t + 1], prod[:], ALU.mult, ALU.add)
+
+        def fetch_sigmoids(c, tag):
+            width = CHUNKS[c][1]
+            sig = keep.tile([P, 2, 2, width], F32, name="sig%d" % c, tag=tag)
+            for k, lst in enumerate((n1_sb, n2_sb)):
+                for i in range(2):
+                    nc.scalar.activation(sig[:, k, i, :], h2[i][:].indirect(lst[:, list_cols(c)]), ACT.Sigmoid)
+            return sig
+
+        def close_chunk(c, sig, got):
+            j0, width = CHUNKS[c]
+            pair_prod = keep.tile([P, 2, width], F32, name="pair_prod%d" % c, tag="pair_prod%d" % c)
+            pair_sum = keep.tile([P, 2, width], F32, name="pair_sum%d" % c, tag="pair_sum%d" % c)
+            nc.vector.scalar_tensor_tensor(pair_prod[:], sig[:, 0], 0.5, th_pair[:, :, j0 : j0 + width], ALU.subtract, ALU.mult)
+            prod = first_term(1, c, got)
+            nc.vector.scalar_tensor_tensor(pair_sum[:], sig[:, 1], 0.5, pair_prod[:], ALU.mult, ALU.add)
+            second_term(1, c, got, prod)
+            for i in range(2):
+                nc.vector.tensor_scalar(
+                    z_planes[c][:, 2 + i, :], pair_sum[:, i, :], 0.25, gs_half[:, 2 + i : 3 + i], ALU.subtract, ALU.mult
+                )
 
         def score(c):
             j0, width = CHUNKS[c]
             last = c == len(CHUNKS) - 1
             z_grouped = keep.tile([P, width, PACK], BF16, name="z_grouped%d" % c, tag="z_grouped%d" % c, align_bytes=64)
             dst = z_grouped[:].rearrange("p (g i) t -> p g t i", i=4)
-            src = z_view(j0, width).rearrange("p t (g i) -> p g t i", i=4)
+            src = z_planes[c][:].rearrange("p t (g i) -> p g t i", i=4)
             if last:
                 nc.vector.tensor_copy(dst, src)
             else:
@@ -171,15 +189,22 @@ def tile_picked_candtanh_none_p_kernel(tc, x_words, x_scales, w1, gs, offs, n1, 
                     nc.scalar.activation(res[:], acc[:], ACT.Copy, scale=0.0625)
                 nc.sync.dma_start(out_rows[:, 2 * pair : 2 * pair + 2, j0 : j0 + width], res[:])
 
-        steps = [(t, half * (S // 2), S // 2) for t in (0, 1) for half in range(2)]
-        steps = steps + [(t, j0, width) for j0, width in CHUNKS for t in (2, 3)]
-        first_term(0, *steps[0])
-        for step, (t, j0, width) in enumerate(steps):
-            if t == PACK - 1:
-                second_term(step, t, j0, width)
-                score(CHUNKS.index((j0, width)))
-                if step + 1 < len(steps):
-                    first_term(step + 1, *steps[step + 1])
-            else:
-                first_term(step + 1, *steps[step + 1])
-                second_term(step, t, j0, width)
+        sig = fetch_sigmoids(0, "sig0")
+        got_a = fetch_th(0, 0, ("a0", "a1"))
+        got_b = fetch_th(0, 1, ("b0", "b1"))
+        prod_a = first_term(0, 0, got_a)
+        prod_b = first_term(0, 1, got_b)
+        second_term(0, 0, got_a, prod_a)
+        second_term(0, 1, got_b, prod_b)
+        close_chunk(0, sig, fetch_th(1, 0, ("c0", "c1")))
+        sig = fetch_sigmoids(1, "sig1")
+        score(0)
+        close_chunk(1, sig, fetch_th(1, 1, ("sig0", "pair_prod0")))
+        score(1)
+        sig = fetch_sigmoids(2, "z_planes0")
+        got_a = fetch_th(0, 2, ("sig1", "pair_prod1"))
+        prod_a = first_term(0, 2, got_a)
+        got_b = fetch_th(1, 2, ("pair_sum0", "pair_sum1"))
+        second_term(0, 2, got_a, prod_a)
+        close_chunk(2, sig, got_b)
+        score(2)

from contextlib import ExitStack

import concourse.mybir as mybir

K, T, S, H, C = 512, 2048, 512, 512, 512
FLOPS = 2 * K * H * S + 2 * K * C * S

F32 = mybir.dt.float32
BF16 = mybir.dt.bfloat16
I32 = mybir.dt.int32
U32 = mybir.dt.uint32
U16 = mybir.dt.uint16
U8 = mybir.dt.uint8
FP8X4 = mybir.dt.float8_e4m3fn_x4
ACT = mybir.ActivationFunctionType
ALU = mybir.AluOpType

P = 128
PACK = 4
LIST_ROWS = 16
CHUNKS = ((0, 256), (256, 128), (384, 128))


def tile_picked_candtanh_none_p_kernel(tc, x_words, x_scales, w1, gs, offs, n1, n2, cand, out):
    nc = tc.nc
    with ExitStack() as ctx:
        keep = ctx.enter_context(tc.tile_pool(name="keep", bufs=1))
        psum = ctx.enter_context(tc.psum_pool(name="psum", bufs=1))

        offs_sb = keep.tile([P, S // LIST_ROWS], U16, name="offs_sb")
        cand_sb = keep.tile([P, C // LIST_ROWS], U16, name="cand_sb")
        n1_sb = keep.tile([P, S // LIST_ROWS], U16, name="n1_sb")
        n2_sb = keep.tile([P, S // LIST_ROWS], U16, name="n2_sb")
        x_word_table = keep.tile([P, T], U32, name="x_word_table", align_bytes=64)
        x_scale_table = keep.tile([P, T], U8, name="x_scale_table", align_bytes=64)
        gs_sb = keep.tile([P, PACK], F32, name="gs_sb")
        gs_half = keep.tile([P, PACK], F32, name="gs_half")
        warm = keep.tile([P, 1], F32, name="warm")
        warm_out = keep.tile([P, 1], F32, name="warm_out")
        w_raw = [keep.tile([P, PACK, H // 2], F32, name="w_raw%d" % half) for half in range(2)]

        nc.vector.memset(x_scale_table[:].bitcast(I32), 0)
        nc.vector.memset(warm[:], 0.0)
        nc.sync.dma_start(offs_sb[:], offs)
        nc.sync.dma_start(cand_sb[:], cand)
        w_rows = w1.rearrange("(p j) c -> p j c", j=PACK)
        nc.sync.dma_start(w_raw[0][:], w_rows[:, :, : H // 2])
        for quad in range(4):
            nc.sync.dma_start(
                x_scale_table[32 * quad : 32 * quad + 4, :].bitcast(I32),
                x_scales[0, 4 * quad : 4 * quad + 4, :].bitcast(I32),
            )
        nc.sync.dma_start(w_raw[1][:], w_rows[:, :, H // 2 :])
        nc.sync.dma_start(x_word_table[:].bitcast(I32), x_words[0].rearrange("p n t -> p (n t)").bitcast(I32))
        nc.sync.dma_start(gs_sb[:], gs.rearrange("(p t) o -> p (t o)", t=PACK))
        nc.sync.dma_start(n1_sb[:], n1)
        nc.sync.dma_start(n2_sb[:], n2)
        nc.scalar.activation(warm_out[:], warm[:], ACT.Sigmoid)
        nc.scalar.activation(gs_half[:, :2], gs_sb[:, :2], ACT.Copy, scale=0.5)
        nc.scalar.activation(gs_half[:, 2:], gs_sb[:, 2:], ACT.Copy, scale=2.0)

        pick_words = keep.tile([P, S], U32, name="pick_words", align_bytes=64)
        pick_scales = keep.tile([P, S], U8, name="pick_scales", align_bytes=64)
        cand_words = keep.tile([P, C], U32, name="cand_words", align_bytes=64)
        cand_scales = keep.tile([P, C], U8, name="cand_scales", align_bytes=64)
        nc.vector.tensor_copy(pick_scales[:], x_scale_table[:].indirect(offs_sb[:]))
        nc.vector.tensor_copy(cand_scales[:], x_scale_table[:].indirect(cand_sb[:]))

        w_grouped = keep.tile([P, PACK, P, PACK], BF16, name="w_grouped", align_bytes=64)
        for half in range(2):
            src = w_raw[half][:].rearrange("p j (m t) -> p m j t", t=PACK)
            dst = w_grouped[:, :, half * (P // 2) : (half + 1) * (P // 2), :].rearrange("p t m j -> p m j t")
            nc.scalar.copy(dst, src)
        w_codes = keep.tile([P, H], U32, name="w_codes", align_bytes=64)
        w_scales = keep.tile([P, H], U8, name="w_scales", align_bytes=64)
        nc.vector.quantize_mx(
            out=w_codes[:].bitcast(FP8X4), scales=w_scales[:], in_=w_grouped[:].rearrange("p t m j -> p (t m j)")
        )

        for half in range(2):
            cols = slice(half * (S // 2), (half + 1) * (S // 2))
            lcols = slice(half * (S // 2) // LIST_ROWS, (half + 1) * (S // 2) // LIST_ROWS)
            nc.vector.tensor_copy(pick_words[:, cols], x_word_table[:].indirect(offs_sb[:, lcols]))
        nc.vector.tensor_copy(cand_words[:], x_word_table[:].indirect(cand_sb[:]))

        th = [keep.tile([P, S], F32, name="th%d" % t) for t in range(2)]
        th_pair = keep.tile([P, 2, S], F32, name="th_pair")
        h2 = [keep.tile([P, S], F32, name="h2_%d" % i) for i in range(2)]

        def project(t, j0, width, bank):
            h_ps = psum.tile([P, width], F32, name="h_ps%d_%d" % (t, j0), tag="bank%d" % bank)
            nc.tensor.matmul_mx(
                out=h_ps[:],
                lhsT=w_codes[:, t * P : (t + 1) * P].bitcast(FP8X4),
                lhsT_scale=w_scales[:, t * P : (t + 1) * P],
                rhs=pick_words[:, j0 : j0 + width].bitcast(FP8X4),
                rhs_scale=pick_scales[:, j0 : j0 + width],
                start=True,
                stop=True,
            )
            if t < 2:
                nc.scalar.activation(th[t][:, j0 : j0 + width], h_ps[:], ACT.Tanh)
            else:
                nc.scalar.activation(h2[t - 2][:], h_ps[:], ACT.Copy, scale=2.0)
                nc.scalar.activation(th_pair[:, t - 2, :], h_ps[:], ACT.Tanh)

        for half in range(2):
            project(0, half * (S // 2), S // 2, 4 * half)
        for t in range(1, PACK):
            project(t, 0, S, t)

        z_planes = [keep.tile([P, PACK, width], F32, name="z_planes%d" % c, tag="z_planes%d" % c) for c, (j0, width) in enumerate(CHUNKS)]
        out_rows = out.rearrange("(b p) j -> p b j", p=P)

        def list_cols(c):
            j0, width = CHUNKS[c]
            return slice(j0 // LIST_ROWS, (j0 + width) // LIST_ROWS)

        def fetch_th(t, c, tags):
            width = CHUNKS[c][1]
            got = []
            for lst, tag in zip((n1_sb, n2_sb), tags):
                got.append(keep.tile([P, width], F32, name="got_" + tag, tag=tag))
                nc.vector.tensor_copy(got[-1][:], th[t][:].indirect(lst[:, list_cols(c)]))
            return got

        def first_term(t, c, got):
            j0, width = CHUNKS[c]
            prod = keep.tile([P, width], F32, name="prod%d_%d" % (t, c))
            nc.vector.scalar_tensor_tensor(prod[:], got[0][:], gs_sb[:, t : t + 1], th[t][:, j0 : j0 + width], ALU.mult, ALU.mult)
            return prod

        def second_term(t, c, got, prod):
            nc.vector.scalar_tensor_tensor(z_planes[c][:, t, :], got[1][:], gs_half[:, t : t + 1], prod[:], ALU.mult, ALU.add)

        def fetch_sigmoids(c, tag):
            width = CHUNKS[c][1]
            sig = keep.tile([P, 2, 2, width], F32, name="sig%d" % c, tag=tag)
            for k, lst in enumerate((n1_sb, n2_sb)):
                for i in range(2):
                    nc.scalar.activation(sig[:, k, i, :], h2[i][:].indirect(lst[:, list_cols(c)]), ACT.Sigmoid)
            return sig

        def close_chunk(c, sig, got):
            j0, width = CHUNKS[c]
            pair_prod = keep.tile([P, 2, width], F32, name="pair_prod%d" % c, tag="pair_prod%d" % c)
            pair_sum = keep.tile([P, 2, width], F32, name="pair_sum%d" % c, tag="pair_sum%d" % c)
            nc.vector.scalar_tensor_tensor(pair_prod[:], sig[:, 0], 0.5, th_pair[:, :, j0 : j0 + width], ALU.subtract, ALU.mult)
            prod = first_term(1, c, got)
            nc.vector.scalar_tensor_tensor(pair_sum[:], sig[:, 1], 0.5, pair_prod[:], ALU.mult, ALU.add)
            second_term(1, c, got, prod)
            for i in range(2):
                nc.vector.tensor_scalar(
                    z_planes[c][:, 2 + i, :], pair_sum[:, i, :], 0.25, gs_half[:, 2 + i : 3 + i], ALU.subtract, ALU.mult
                )

        def score(c):
            j0, width = CHUNKS[c]
            last = c == len(CHUNKS) - 1
            z_grouped = keep.tile([P, width, PACK], BF16, name="z_grouped%d" % c, tag="z_grouped%d" % c, align_bytes=64)
            dst = z_grouped[:].rearrange("p (g i) t -> p g t i", i=4)
            src = z_planes[c][:].rearrange("p t (g i) -> p g t i", i=4)
            if last:
                nc.vector.tensor_copy(dst, src)
            else:
                nc.scalar.copy(dst, src)
            z_codes = keep.tile([P, width], U32, name="z_codes%d" % c, align_bytes=64)
            z_scales = keep.tile([P, width], U8, name="z_scales%d" % c, align_bytes=64)
            nc.vector.quantize_mx(
                out=z_codes[:].bitcast(FP8X4), scales=z_scales[:], in_=z_grouped[:].rearrange("p n t -> p (n t)")
            )
            for pair in range(2):
                acc = psum.tile([P, 2, width], F32, name="acc%d_%d" % (c, pair), tag="bank%d" % ((5 + 2 * c + pair) % 8))
                for i in range(2):
                    b = 2 * pair + i
                    nc.tensor.matmul_mx(
                        out=acc[:, i, :],
                        lhsT=cand_words[:, b * P : (b + 1) * P].bitcast(FP8X4),
                        lhsT_scale=cand_scales[:, b * P : (b + 1) * P],
                        rhs=z_codes[:].bitcast(FP8X4),
                        rhs_scale=z_scales[:],
                        start=True,
                        stop=True,
                    )
                res = keep.tile([P, 2, width], F32, name="res%d_%d" % (c, pair))
                if last and pair == 1:
                    nc.vector.tensor_scalar(res[:], acc[:], 0.0625, None, ALU.mult)
                else:
                    nc.scalar.activation(res[:], acc[:], ACT.Copy, scale=0.0625)
                nc.sync.dma_start(out_rows[:, 2 * pair : 2 * pair + 2, j0 : j0 + width], res[:])

        sig = fetch_sigmoids(0, "sig0")
        got_a = fetch_th(0, 0, ("a0", "a1"))
        got_b = fetch_th(0, 1, ("b0", "b1"))
        prod_a = first_term(0, 0, got_a)
        prod_b = first_term(0, 1, got_b)
        second_term(0, 0, got_a, prod_a)
        second_term(0, 1, got_b, prod_b)
        close_chunk(0, sig, fetch_th(1, 0, ("c0", "c1")))
        sig = fetch_sigmoids(1, "sig1")
        score(0)
        close_chunk(1, sig, fetch_th(1, 1, ("sig0", "pair_prod0")))
        score(1)
        sig = fetch_sigmoids(2, "z_planes0")
        got_a = fetch_th(0, 2, ("sig1", "pair_prod1"))
        prod_a = first_term(0, 2, got_a)
        got_b = fetch_th(1, 2, ("pair_sum0", "pair_sum1"))
        second_term(0, 2, got_a, prod_a)
        close_chunk(2, sig, got_b)
        score(2)
